import numpy as np
import ml_dtypes


def mxq(x, axis, fmt="e4m3"):
    dtype, down = {"e4m3": (ml_dtypes.float8_e4m3fn, 7), "e5m2": (ml_dtypes.float8_e5m2, 14)}[fmt]
    v = np.moveaxis(np.asarray(x, np.float32).astype(ml_dtypes.bfloat16).astype(np.float64), axis, -1)
    blocks = v.reshape(v.shape[:-1] + (-1, 32))
    amax = np.abs(blocks).max(-1, keepdims=True)
    byte = np.maximum(np.where(amax > 0, np.frexp(amax)[1] - 1 + 127, 0) - down, 1)
    scale = np.exp2(byte - 127.0)
    codes = (blocks / scale).astype(np.float32).astype(dtype).astype(np.float64)
    return np.moveaxis((codes * scale).reshape(v.shape), -1, axis)


WIDE = False


def mx_kscale(k):
    if not WIDE:
        return np.ones(k)
    levels = np.array([10, -10, 5, -5, 0])
    if k % 512:
        return np.exp2(np.random.permutation(np.resize(levels, k // 32))).repeat(32)
    a = np.empty((k // 512, 16))
    for p in range(k // 512):
        a[p, :8] = np.random.permutation(np.resize(levels, 8))
        for g in range(8):
            far = levels[np.abs(levels - a[p, g]) >= 10]
            a[p, g + 8] = far[np.random.randint(len(far))]
    return np.exp2(a.ravel()).repeat(32)


def f64(x):
    return np.asarray(x).astype(np.float64)


def striped8(idx):
    return np.asarray(idx).reshape(8, -1, 16).transpose(0, 2, 1).reshape(128, -1).astype(np.uint16)


def unstriped8(offs):
    return offs.reshape(8, 16, -1).transpose(0, 2, 1).reshape(8, -1).astype(np.int64)


def pick8(x, idx, run):
    r = np.arange(len(x))
    return x[r[:, None], idx[r % (8 * run) // run]]


E2M1 = np.array([0.0, 0.5, 1.0, 1.5, 2.0, 3.0, 4.0, 6.0, -0.0, -0.5, -1.0, -1.5, -2.0, -3.0, -4.0, -6.0])


def pack_weight(w, fmt):
    k, n = w.shape
    w = f64(np.asarray(w, np.float32).astype(ml_dtypes.bfloat16)).reshape(k // 32, 32, n)
    amax = np.abs(w).max(1)
    if fmt == "e4m3":
        byte = np.frexp(amax)[1] - 1 + 127 - 7
    else:
        mant, ex = np.frexp(amax / 6.0)
        byte = np.where(mant > 0.5, ex, ex - 1) + 127
    byte = np.clip(np.where(amax > 0, byte, 1), 1, 254)
    scaled = (w * np.exp2(127.0 - byte)[:, None, :]).reshape(k, n).astype(np.float32)
    by_word = np.ascontiguousarray(scaled.reshape(k // 512, 128, 4, n).transpose(0, 1, 3, 2))
    if fmt == "e4m3":
        words = by_word.astype(ml_dtypes.float8_e4m3fn).view(np.uint8)
    else:
        c = by_word.astype(ml_dtypes.float4_e2m1fn).view(np.uint8) & 0xF
        words = (c[..., 0::2] | (c[..., 1::2] << 4)).reshape(k // 512, 128, 2 * n)
    return np.ascontiguousarray(words), np.ascontiguousarray(byte.astype(np.uint8).reshape(k // 512, 16, n))


def unpack_weight(words, scales, fmt):
    g, _, n = scales.shape
    words = np.ascontiguousarray(words).reshape(g, 128, n, -1)
    if fmt == "e4m3":
        vals = words.view(ml_dtypes.float8_e4m3fn).astype(np.float64)
    else:
        nib = np.empty((g, 128, n, 4), np.uint8)
        nib[..., 0::2] = words & 0xF
        nib[..., 1::2] = words >> 4
        vals = E2M1[nib]
    vals = vals * np.repeat(np.exp2(scales.astype(np.float64) - 127.0), 8, axis=1)[..., None]
    return vals.transpose(0, 1, 3, 2).reshape(g * 512, n)


D, T, I, Q = 512, 1024, 512, 128


def setup_inputs():
    n = np.random.standard_normal
    idx = np.stack([np.random.permutation(T)[:I] for _ in range(8)])
    idx2 = np.stack([np.random.permutation(T)[:I] for _ in range(8)])
    idx3 = np.stack([np.random.permutation(T)[:I] for _ in range(8)])
    idx4 = np.stack([np.random.permutation(T)[:I] for _ in range(8)])
    fd = mx_kscale(D)
    keysp = pack_weight(n((D, T)) / fd[:, None], "e2m1")
    return {
        "query": (n((D, Q)) * 1.0 / np.sqrt(D) * fd[:, None]).astype(np.float32),
        "keys_words": keysp[0],
        "keys_scales": keysp[1],
        "lam": (np.random.uniform(0.5, 1.5, (Q, 1))).astype(np.float32),
        "offs": striped8(idx),
        "offs2": striped8(idx2),
        "offs3": striped8(idx3),
        "offs4": striped8(idx4),
    }


def reference(query, keys_words, keys_scales, lam, offs, offs2, offs3, offs4):
    idx = unstriped8(offs)
    idx2 = unstriped8(offs2)
    idx3 = unstriped8(offs3)
    idx4 = unstriped8(offs4)
    keysu = unpack_weight(keys_words, keys_scales, "e2m1")
    queryq = mxq(f64(query), 0, "e4m3")
    a = queryq.T @ keysu
    w = np.maximum(pick8(a, idx2, 16), pick8(a, idx3, 16))
    f1 = np.zeros((Q, T))
    f1[np.arange(Q)[:, None], idx[np.arange(Q) % 128 // 16]] = w
    cc = a - f1 * f64(lam)
    tc2 = np.max(cc, axis=1, keepdims=True)
    y = np.exp(pick8(cc, idx4, 16) - tc2)
    return y

@@ -1,0 +1,119 @@
+from contextlib import ExitStack
+
+import concourse.mybir as mybir
+
+D, T, I, Q = 512, 1024, 512, 128
+FLOPS = 2 * D * T * Q
+
+F32 = mybir.dt.float32
+BF16 = mybir.dt.bfloat16
+I32 = mybir.dt.int32
+U32 = mybir.dt.uint32
+U16 = mybir.dt.uint16
+U8 = mybir.dt.uint8
+FP8X4 = mybir.dt.float8_e4m3fn_x4
+FP4X4 = mybir.dt.float4_e2m1fn_x4
+ALU = mybir.AluOpType
+ACT = mybir.ActivationFunctionType
+
+P = 128
+PACK = 4
+HALF = I // 2
+LIST_COLS = HALF // 16
+SPLIT = 704
+PASSES = ((0, 512, "scalar"), (512, 256, "vector"), (768, 128, "scalar"), (896, 128, "vector"))
+
+
+def tile_attend_shadowed_one_kernel(tc, query, keys_words, keys_scales, lam, offs, offs2, offs3, offs4, out):
+    nc = tc.nc
+    with ExitStack() as ctx:
+        lists = ctx.enter_context(tc.tile_pool(name="lists", bufs=1))
+        sb = ctx.enter_context(tc.tile_pool(name="sb", bufs=1))
+        psum = ctx.enter_context(tc.psum_pool(name="psum", bufs=1))
+
+        key_scales = sb.tile([P, T], U8, name="key_scales", align_bytes=64)
+        nc.vector.memset(key_scales[:].bitcast(I32), 0)
+
+        q_raw = sb.tile([P, PACK, Q], F32, name="q_raw")
+        nc.sync.dma_start(q_raw[:], query.rearrange("(p j) q -> p j q", j=PACK))
+        key_words = [sb.tile([P, T], U8, name=f"key_words{h}", align_bytes=64) for h in range(2)]
+        nc.sync.dma_start(key_words[0][:].bitcast(I32), keys_words[0, :, 0:T].bitcast(I32))
+        for quad in range(4):
+            nc.sync.dma_start(
+                key_scales[32 * quad : 32 * quad + 4, :].bitcast(I32),
+                keys_scales[0, 4 * quad : 4 * quad + 4, :].bitcast(I32),
+            )
+        nc.sync.dma_start(key_words[1][:].bitcast(I32), keys_words[0, :, T : 2 * T].bitcast(I32))
+        list2 = lists.tile([P, I // 16], U16, name="list2")
+        nc.sync.dma_start(list2[:], offs2)
+        list3 = lists.tile([P, I // 16], U16, name="list3")
+        nc.sync.dma_start(list3[:], offs3)
+        list1 = lists.tile([P, I // 16], U16, name="list1")
+        nc.sync.dma_start(list1[:], offs)
+        list4 = lists.tile([P, I // 16], U16, name="list4")
+        nc.sync.dma_start(list4[:], offs4)
+        lam_col = sb.tile([P, 1], F32, name="lam_col")
+        nc.gpsimd.dma_start(lam_col[:], lam)
+
+        f1 = sb.tile([P, T], F32, name="f1")
+        nc.vector.memset(f1[:], 0.0)
+
+        q_bf = sb.tile([P, Q, PACK], BF16, name="q_bf", tag="kib", align_bytes=64)
+        q_codes = sb.tile([P, Q], U32, name="q_codes", align_bytes=64)
+        q_scales = sb.tile([P, Q], U8, name="q_scales", align_bytes=64)
+        row_halves = (slice(0, Q // 2), slice(Q // 2, Q))
+        for rows in row_halves:
+            nc.vector.tensor_copy(q_bf[:, rows, :], q_raw[:, :, rows].rearrange("p j q -> p q j"))
+        for rows in row_halves:
+            nc.vector.quantize_mx(
+                out=q_codes[:, rows].bitcast(FP8X4),
+                scales=q_scales[:, rows],
+                in_=q_bf[:, rows, :].rearrange("p q j -> p (q j)"),
+            )
+        lam_wide = sb.tile([P, HALF], F32, name="lam_wide", tag="kib", align_bytes=64)
+        nc.gpsimd.tensor_scalar(lam_wide[:], lam_col[:].to_broadcast([P, HALF]), 1.0, 0.0, ALU.mult, ALU.add)
+
+        a = sb.tile([P, T], F32, name="a")
+        banks = []
+        for first, width, engine in PASSES:
+            bank = psum.tile([P, width], F32, name=f"bank{first}")
+            banks.append(bank)
+            nc.tensor.matmul_mx(
+                out=bank[:],
+                lhsT=q_codes[:].bitcast(FP8X4),
+                lhsT_scale=q_scales[:],
+                rhs=key_words[first // 512][:, 2 * (first % 512) : 2 * (first % 512 + width)].bitcast(FP4X4),
+                rhs_scale=key_scales[:, first : first + width],
+                start=True,
+                stop=True,
+            )
+            if engine == "scalar":
+                nc.scalar.activation(a[:, first : first + width], bank[:], ACT.Copy)
+            else:
+                nc.vector.tensor_copy(a[:, first : first + width], bank[:])
+
+        for half in range(2):
+            cols = slice(half * LIST_COLS, (half + 1) * LIST_COLS)
+            g2 = sb.tile([P, HALF], F32, name=f"g2_{half}")
+            g3 = sb.tile([P, HALF], F32, name=f"g3_{half}")
+            if half == 0:
+                nc.vector.tensor_copy(g2[:], a[:].indirect(list2[:, cols]))
+            else:
+                nc.scalar.activation(g2[:], a[:].indirect(list2[:, cols]), ACT.Copy)
+            nc.scalar.activation(g3[:], a[:].indirect(list3[:, cols]), ACT.Copy)
+            w = sb.tile([P, HALF], F32, name=f"w_{half}")
+            nc.vector.tensor_tensor(w[:], g2[:], g3[:], ALU.max)
+            nc.vector.tensor_tensor(f1[:].indirect(list1[:, cols]), w[:], lam_wide[:], ALU.mult)
+
+        cc = sb.tile([P, T], F32, name="cc")
+        nc.gpsimd.tensor_tensor(cc[:, SPLIT:], a[:, SPLIT:], f1[:, SPLIT:], ALU.subtract)
+        nc.vector.tensor_tensor(cc[:, 0:512], banks[0][:], f1[:, 0:512], ALU.subtract)
+        nc.vector.tensor_tensor(cc[:, 512:SPLIT], banks[1][:, 0 : SPLIT - 512], f1[:, 512:SPLIT], ALU.subtract)
+        neg_top = sb.tile([P, 1], F32, name="neg_top")
+        nc.vector.tensor_reduce(neg_top[:], cc[:], mybir.AxisListType.X, ALU.max, negate=True)
+
+        for half in range(2):
+            cols = slice(half * LIST_COLS, (half + 1) * LIST_COLS)
+            y = sb.tile([P, HALF], F32, name=f"y_{half}")
+            nc.scalar.activation(y[:], cc[:].indirect(list4[:, cols]), ACT.Exp, bias=neg_top[:])
+            nc.sync.dma_start(out[:, half * HALF : (half + 1) * HALF], y[:])

@@ -53,7 +53,7 @@ def tile_attend_shadowed_one_kernel(tc, query, keys_words, keys_scales, lam, off
         list4 = lists.tile([P, I // 16], U16, name="list4")
         nc.sync.dma_start(list4[:], offs4)
         lam_col = sb.tile([P, 1], F32, name="lam_col")
-        nc.gpsimd.dma_start(lam_col[:], lam)
+        nc.sync.dma_start(lam_col[:], lam)
 
         f1 = sb.tile([P, T], F32, name="f1")
         nc.vector.memset(f1[:], 0.0)
@@ -116,4 +116,5 @@ def tile_attend_shadowed_one_kernel(tc, query, keys_words, keys_scales, lam, off
             cols = slice(half * LIST_COLS, (half + 1) * LIST_COLS)
             y = sb.tile([P, HALF], F32, name=f"y_{half}")
             nc.scalar.activation(y[:], cc[:].indirect(list4[:, cols]), ACT.Exp, bias=neg_top[:])
-            nc.sync.dma_start(out[:, half * HALF : (half + 1) * HALF], y[:])
+            queue = nc.sync if half == 0 else nc.scalar
+            queue.dma_start(out[:, half * HALF : (half + 1) * HALF], y[:])

@@ -20,7 +20,7 @@ P = 128
 PACK = 4
 HALF = I // 2
 LIST_COLS = HALF // 16
-SPLIT = 704
+SPLIT = 736
 PASSES = ((0, 512, "scalar"), (512, 256, "vector"), (768, 128, "scalar"), (896, 128, "vector"))
 
 
@@ -38,11 +38,8 @@ def tile_attend_shadowed_one_kernel(tc, query, keys_words, keys_scales, lam, off
         nc.sync.dma_start(q_raw[:], query.rearrange("(p j) q -> p j q", j=PACK))
         key_words = [sb.tile([P, T], U8, name=f"key_words{h}", align_bytes=64) for h in range(2)]
         nc.sync.dma_start(key_words[0][:].bitcast(I32), keys_words[0, :, 0:T].bitcast(I32))
-        for quad in range(4):
-            nc.sync.dma_start(
-                key_scales[32 * quad : 32 * quad + 4, :].bitcast(I32),
-                keys_scales[0, 4 * quad : 4 * quad + 4, :].bitcast(I32),
-            )
+        for row in range(4):
+            nc.sync.dma_start(key_scales[row:P:32, :].bitcast(I32), keys_scales[0, row:16:4, :].bitcast(I32))
         nc.sync.dma_start(key_words[1][:].bitcast(I32), keys_words[0, :, T : 2 * T].bitcast(I32))
         list2 = lists.tile([P, I // 16], U16, name="list2")
         nc.sync.dma_start(list2[:], offs2)
@@ -53,12 +50,12 @@ def tile_attend_shadowed_one_kernel(tc, query, keys_words, keys_scales, lam, off
         list4 = lists.tile([P, I // 16], U16, name="list4")
         nc.sync.dma_start(list4[:], offs4)
         lam_col = sb.tile([P, 1], F32, name="lam_col")
-        nc.sync.dma_start(lam_col[:], lam)
+        nc.gpsimd.dma_start(lam_col[:], lam)
 
         f1 = sb.tile([P, T], F32, name="f1")
         nc.vector.memset(f1[:], 0.0)
 
-        q_bf = sb.tile([P, Q, PACK], BF16, name="q_bf", tag="kib", align_bytes=64)
+        q_bf = sb.tile([P, Q, PACK], BF16, name="q_bf", align_bytes=64)
         q_codes = sb.tile([P, Q], U32, name="q_codes", align_bytes=64)
         q_scales = sb.tile([P, Q], U8, name="q_scales", align_bytes=64)
         row_halves = (slice(0, Q // 2), slice(Q // 2, Q))
@@ -70,8 +67,8 @@ def tile_attend_shadowed_one_kernel(tc, query, keys_words, keys_scales, lam, off
                 scales=q_scales[:, rows],
                 in_=q_bf[:, rows, :].rearrange("p q j -> p (q j)"),
             )
-        lam_wide = sb.tile([P, HALF], F32, name="lam_wide", tag="kib", align_bytes=64)
-        nc.gpsimd.tensor_scalar(lam_wide[:], lam_col[:].to_broadcast([P, HALF]), 1.0, 0.0, ALU.mult, ALU.add)
+        neg_lam = sb.tile([P, 1], F32, name="neg_lam")
+        nc.gpsimd.tensor_scalar(neg_lam[:], lam_col[:], -1.0, 0.0, ALU.mult, ALU.add)
 
         a = sb.tile([P, T], F32, name="a")
         banks = []
@@ -103,12 +100,10 @@ def tile_attend_shadowed_one_kernel(tc, query, keys_words, keys_scales, lam, off
             nc.scalar.activation(g3[:], a[:].indirect(list3[:, cols]), ACT.Copy)
             w = sb.tile([P, HALF], F32, name=f"w_{half}")
             nc.vector.tensor_tensor(w[:], g2[:], g3[:], ALU.max)
-            nc.vector.tensor_tensor(f1[:].indirect(list1[:, cols]), w[:], lam_wide[:], ALU.mult)
+            nc.vector.tensor_copy(f1[:].indirect(list1[:, cols]), w[:])
 
         cc = sb.tile([P, T], F32, name="cc")
-        nc.gpsimd.tensor_tensor(cc[:, SPLIT:], a[:, SPLIT:], f1[:, SPLIT:], ALU.subtract)
-        nc.vector.tensor_tensor(cc[:, 0:512], banks[0][:], f1[:, 0:512], ALU.subtract)
-        nc.vector.tensor_tensor(cc[:, 512:SPLIT], banks[1][:, 0 : SPLIT - 512], f1[:, 512:SPLIT], ALU.subtract)
+        nc.vector.scalar_tensor_tensor(cc[:], f1[:], neg_lam[:], a[:], ALU.mult, ALU.add)
         neg_top = sb.tile([P, 1], F32, name="neg_top")
         nc.vector.tensor_reduce(neg_top[:], cc[:], mybir.AxisListType.X, ALU.max, negate=True)
 
@@ -116,5 +111,4 @@ def tile_attend_shadowed_one_kernel(tc, query, keys_words, keys_scales, lam, off
             cols = slice(half * LIST_COLS, (half + 1) * LIST_COLS)
             y = sb.tile([P, HALF], F32, name=f"y_{half}")
             nc.scalar.activation(y[:], cc[:].indirect(list4[:, cols]), ACT.Exp, bias=neg_top[:])
-            queue = nc.sync if half == 0 else nc.scalar
-            queue.dma_start(out[:, half * HALF : (half + 1) * HALF], y[:])
+            nc.sync.dma_start(out[:, half * HALF : (half + 1) * HALF], y[:])

@@ -18,10 +18,20 @@ ACT = mybir.ActivationFunctionType
 
 P = 128
 PACK = 4
-HALF = I // 2
-LIST_COLS = HALF // 16
-SPLIT = 736
+QUADRANT = 32
+PER_COLUMN = 16
+HALF_SLOTS = I // 2
+HALF_TOKENS = T // 2
+
 PASSES = ((0, 512, "scalar"), (512, 256, "vector"), (768, 128, "scalar"), (896, 128, "vector"))
+
+FIRST_SLOTS = 128
+
+VECTOR_COLUMNS = 704
+
+
+def list_columns(first_slot, end_slot):
+    return slice(first_slot // PER_COLUMN, end_slot // PER_COLUMN)
 
 
 def tile_attend_shadowed_one_kernel(tc, query, keys_words, keys_scales, lam, offs, offs2, offs3, offs4, out):
@@ -36,26 +46,27 @@ def tile_attend_shadowed_one_kernel(tc, query, keys_words, keys_scales, lam, off
 
         q_raw = sb.tile([P, PACK, Q], F32, name="q_raw")
         nc.sync.dma_start(q_raw[:], query.rearrange("(p j) q -> p j q", j=PACK))
-        key_words = [sb.tile([P, T], U8, name=f"key_words{h}", align_bytes=64) for h in range(2)]
-        nc.sync.dma_start(key_words[0][:].bitcast(I32), keys_words[0, :, 0:T].bitcast(I32))
+        half_bytes = 2 * HALF_TOKENS
+        key_words = [sb.tile([P, half_bytes], U8, name=f"key_words{h}", align_bytes=64) for h in range(2)]
+        nc.sync.dma_start(key_words[0][:].bitcast(I32), keys_words[0, :, 0:half_bytes].bitcast(I32))
         for row in range(4):
-            nc.sync.dma_start(key_scales[row:P:32, :].bitcast(I32), keys_scales[0, row:16:4, :].bitcast(I32))
-        nc.sync.dma_start(key_words[1][:].bitcast(I32), keys_words[0, :, T : 2 * T].bitcast(I32))
-        list2 = lists.tile([P, I // 16], U16, name="list2")
+            nc.sync.dma_start(key_scales[row:P:QUADRANT, :].bitcast(I32), keys_scales[0, row:16:4, :].bitcast(I32))
+        nc.sync.dma_start(key_words[1][:].bitcast(I32), keys_words[0, :, half_bytes : 2 * half_bytes].bitcast(I32))
+        list2 = lists.tile([P, I // PER_COLUMN], U16, name="list2")
         nc.sync.dma_start(list2[:], offs2)
-        list3 = lists.tile([P, I // 16], U16, name="list3")
+        list3 = lists.tile([P, I // PER_COLUMN], U16, name="list3")
         nc.sync.dma_start(list3[:], offs3)
-        list1 = lists.tile([P, I // 16], U16, name="list1")
+        list1 = lists.tile([P, I // PER_COLUMN], U16, name="list1")
         nc.sync.dma_start(list1[:], offs)
-        list4 = lists.tile([P, I // 16], U16, name="list4")
+        list4 = lists.tile([P, I // PER_COLUMN], U16, name="list4")
         nc.sync.dma_start(list4[:], offs4)
         lam_col = sb.tile([P, 1], F32, name="lam_col")
         nc.gpsimd.dma_start(lam_col[:], lam)
 
-        f1 = sb.tile([P, T], F32, name="f1")
-        nc.vector.memset(f1[:], 0.0)
+        shadow = sb.tile([P, T], F32, name="shadow")
+        nc.vector.memset(shadow[:], 0.0)
 
-        q_bf = sb.tile([P, Q, PACK], BF16, name="q_bf", align_bytes=64)
+        q_bf = sb.tile([P, Q, PACK], BF16, name="q_bf", tag="q_bf_then_lam", align_bytes=64)
         q_codes = sb.tile([P, Q], U32, name="q_codes", align_bytes=64)
         q_scales = sb.tile([P, Q], U8, name="q_scales", align_bytes=64)
         row_halves = (slice(0, Q // 2), slice(Q // 2, Q))
@@ -67,19 +78,22 @@ def tile_attend_shadowed_one_kernel(tc, query, keys_words, keys_scales, lam, off
                 scales=q_scales[:, rows],
                 in_=q_bf[:, rows, :].rearrange("p q j -> p (q j)"),
             )
-        neg_lam = sb.tile([P, 1], F32, name="neg_lam")
-        nc.gpsimd.tensor_scalar(neg_lam[:], lam_col[:], -1.0, 0.0, ALU.mult, ALU.add)
+
+        rest_slots = I - FIRST_SLOTS
+        lam_wide = sb.tile([P, rest_slots], F32, name="lam_wide", tag="q_bf_then_lam", align_bytes=64)
+        nc.gpsimd.tensor_scalar(lam_wide[:], lam_col[:].to_broadcast([P, rest_slots]), 1.0, 0.0, ALU.mult, ALU.add)
 
         a = sb.tile([P, T], F32, name="a")
         banks = []
         for first, width, engine in PASSES:
             bank = psum.tile([P, width], F32, name=f"bank{first}")
             banks.append(bank)
+            within = first % HALF_TOKENS
             nc.tensor.matmul_mx(
                 out=bank[:],
                 lhsT=q_codes[:].bitcast(FP8X4),
                 lhsT_scale=q_scales[:],
-                rhs=key_words[first // 512][:, 2 * (first % 512) : 2 * (first % 512 + width)].bitcast(FP4X4),
+                rhs=key_words[first // HALF_TOKENS][:, 2 * within : 2 * (within + width)].bitcast(FP4X4),
                 rhs_scale=key_scales[:, first : first + width],
                 start=True,
                 stop=True,
@@ -89,26 +103,42 @@ def tile_attend_shadowed_one_kernel(tc, query, keys_words, keys_scales, lam, off
             else:
                 nc.vector.tensor_copy(a[:, first : first + width], bank[:])
 
-        for half in range(2):
-            cols = slice(half * LIST_COLS, (half + 1) * LIST_COLS)
-            g2 = sb.tile([P, HALF], F32, name=f"g2_{half}")
-            g3 = sb.tile([P, HALF], F32, name=f"g3_{half}")
-            if half == 0:
-                nc.vector.tensor_copy(g2[:], a[:].indirect(list2[:, cols]))
-            else:
-                nc.scalar.activation(g2[:], a[:].indirect(list2[:, cols]), ACT.Copy)
-            nc.scalar.activation(g3[:], a[:].indirect(list3[:, cols]), ACT.Copy)
-            w = sb.tile([P, HALF], F32, name=f"w_{half}")
-            nc.vector.tensor_tensor(w[:], g2[:], g3[:], ALU.max)
-            nc.vector.tensor_copy(f1[:].indirect(list1[:, cols]), w[:])
+        by2 = [sb.tile([P, HALF_SLOTS], F32, name=f"by2_{h}") for h in range(2)]
+        by3 = [sb.tile([P, HALF_SLOTS], F32, name=f"by3_{h}") for h in range(2)]
+        w = sb.tile([P, I], F32, name="w")
+        first_half, second_half = list_columns(0, HALF_SLOTS), list_columns(HALF_SLOTS, I)
+        nc.vector.tensor_copy(by2[0][:], a[:].indirect(list2[:, first_half]))
+        nc.scalar.activation(by3[0][:], a[:].indirect(list3[:, first_half]), ACT.Copy)
+        nc.scalar.activation(by2[1][:], a[:].indirect(list2[:, second_half]), ACT.Copy)
+        nc.scalar.activation(by3[1][:], a[:].indirect(list3[:, second_half]), ACT.Copy)
+
+        nc.vector.tensor_tensor(w[:, 0:FIRST_SLOTS], by2[0][:, 0:FIRST_SLOTS], by3[0][:, 0:FIRST_SLOTS], ALU.max)
+        nc.vector.tensor_tensor(w[:, FIRST_SLOTS:HALF_SLOTS], by2[0][:, FIRST_SLOTS:], by3[0][:, FIRST_SLOTS:], ALU.max)
+        nc.vector.tensor_tensor(
+            shadow[:].indirect(list1[:, list_columns(0, FIRST_SLOTS)]),
+            w[:, 0:FIRST_SLOTS],
+            lam_wide[:, 0:FIRST_SLOTS],
+            ALU.mult,
+        )
+        nc.vector.tensor_tensor(w[:, HALF_SLOTS:], by2[1][:], by3[1][:], ALU.max)
+        nc.vector.tensor_tensor(
+            shadow[:].indirect(list1[:, list_columns(FIRST_SLOTS, I)]), w[:, FIRST_SLOTS:], lam_wide[:], ALU.mult
+        )
 
         cc = sb.tile([P, T], F32, name="cc")
-        nc.vector.scalar_tensor_tensor(cc[:], f1[:], neg_lam[:], a[:], ALU.mult, ALU.add)
+        nc.gpsimd.tensor_tensor(cc[:, VECTOR_COLUMNS:], a[:, VECTOR_COLUMNS:], shadow[:, VECTOR_COLUMNS:], ALU.subtract)
+        second_first = PASSES[1][0]
+        nc.vector.tensor_tensor(cc[:, 0:second_first], banks[0][:], shadow[:, 0:second_first], ALU.subtract)
+        nc.vector.tensor_tensor(
+            cc[:, second_first:VECTOR_COLUMNS],
+            banks[1][:, 0 : VECTOR_COLUMNS - second_first],
+            shadow[:, second_first:VECTOR_COLUMNS],
+            ALU.subtract,
+        )
         neg_top = sb.tile([P, 1], F32, name="neg_top")
         nc.vector.tensor_reduce(neg_top[:], cc[:], mybir.AxisListType.X, ALU.max, negate=True)
 
-        for half in range(2):
-            cols = slice(half * LIST_COLS, (half + 1) * LIST_COLS)
-            y = sb.tile([P, HALF], F32, name=f"y_{half}")
-            nc.scalar.activation(y[:], cc[:].indirect(list4[:, cols]), ACT.Exp, bias=neg_top[:])
-            nc.sync.dma_start(out[:, half * HALF : (half + 1) * HALF], y[:])
+        for h, columns in enumerate((first_half, second_half)):
+            y = sb.tile([P, HALF_SLOTS], F32, name=f"y_{h}")
+            nc.scalar.activation(y[:], cc[:].indirect(list4[:, columns]), ACT.Exp, bias=neg_top[:])
+            nc.sync.dma_start(out[:, h * HALF_SLOTS : (h + 1) * HALF_SLOTS], y[:])

from contextlib import ExitStack

import concourse.mybir as mybir

D, T, I, Q = 512, 1024, 512, 128
FLOPS = 2 * D * T * Q

F32 = mybir.dt.float32
BF16 = mybir.dt.bfloat16
I32 = mybir.dt.int32
U32 = mybir.dt.uint32
U16 = mybir.dt.uint16
U8 = mybir.dt.uint8
FP8X4 = mybir.dt.float8_e4m3fn_x4
FP4X4 = mybir.dt.float4_e2m1fn_x4
ALU = mybir.AluOpType
ACT = mybir.ActivationFunctionType

P = 128
PACK = 4
QUADRANT = 32
PER_COLUMN = 16
HALF_SLOTS = I // 2
HALF_TOKENS = T // 2

PASSES = ((0, 512, "scalar"), (512, 256, "vector"), (768, 128, "scalar"), (896, 128, "vector"))

FIRST_SLOTS = 128

VECTOR_COLUMNS = 704


def list_columns(first_slot, end_slot):
    return slice(first_slot // PER_COLUMN, end_slot // PER_COLUMN)


def tile_attend_shadowed_one_kernel(tc, query, keys_words, keys_scales, lam, offs, offs2, offs3, offs4, out):
    nc = tc.nc
    with ExitStack() as ctx:
        lists = ctx.enter_context(tc.tile_pool(name="lists", bufs=1))
        sb = ctx.enter_context(tc.tile_pool(name="sb", bufs=1))
        psum = ctx.enter_context(tc.psum_pool(name="psum", bufs=1))

        key_scales = sb.tile([P, T], U8, name="key_scales", align_bytes=64)
        nc.vector.memset(key_scales[:].bitcast(I32), 0)

        q_raw = sb.tile([P, PACK, Q], F32, name="q_raw")
        nc.sync.dma_start(q_raw[:], query.rearrange("(p j) q -> p j q", j=PACK))
        half_bytes = 2 * HALF_TOKENS
        key_words = [sb.tile([P, half_bytes], U8, name=f"key_words{h}", align_bytes=64) for h in range(2)]
        nc.sync.dma_start(key_words[0][:].bitcast(I32), keys_words[0, :, 0:half_bytes].bitcast(I32))
        for row in range(4):
            nc.sync.dma_start(key_scales[row:P:QUADRANT, :].bitcast(I32), keys_scales[0, row:16:4, :].bitcast(I32))
        nc.sync.dma_start(key_words[1][:].bitcast(I32), keys_words[0, :, half_bytes : 2 * half_bytes].bitcast(I32))
        list2 = lists.tile([P, I // PER_COLUMN], U16, name="list2")
        nc.sync.dma_start(list2[:], offs2)
        list3 = lists.tile([P, I // PER_COLUMN], U16, name="list3")
        nc.sync.dma_start(list3[:], offs3)
        list1 = lists.tile([P, I // PER_COLUMN], U16, name="list1")
        nc.sync.dma_start(list1[:], offs)
        list4 = lists.tile([P, I // PER_COLUMN], U16, name="list4")
        nc.sync.dma_start(list4[:], offs4)
        lam_col = sb.tile([P, 1], F32, name="lam_col")
        nc.gpsimd.dma_start(lam_col[:], lam)

        shadow = sb.tile([P, T], F32, name="shadow")
        nc.vector.memset(shadow[:], 0.0)

        q_bf = sb.tile([P, Q, PACK], BF16, name="q_bf", tag="q_bf_then_lam", align_bytes=64)
        q_codes = sb.tile([P, Q], U32, name="q_codes", align_bytes=64)
        q_scales = sb.tile([P, Q], U8, name="q_scales", align_bytes=64)
        row_halves = (slice(0, Q // 2), slice(Q // 2, Q))
        for rows in row_halves:
            nc.vector.tensor_copy(q_bf[:, rows, :], q_raw[:, :, rows].rearrange("p j q -> p q j"))
        for rows in row_halves:
            nc.vector.quantize_mx(
                out=q_codes[:, rows].bitcast(FP8X4),
                scales=q_scales[:, rows],
                in_=q_bf[:, rows, :].rearrange("p q j -> p (q j)"),
            )

        rest_slots = I - FIRST_SLOTS
        lam_wide = sb.tile([P, rest_slots], F32, name="lam_wide", tag="q_bf_then_lam", align_bytes=64)
        nc.gpsimd.tensor_scalar(lam_wide[:], lam_col[:].to_broadcast([P, rest_slots]), 1.0, 0.0, ALU.mult, ALU.add)

        a = sb.tile([P, T], F32, name="a")
        banks = []
        for first, width, engine in PASSES:
            bank = psum.tile([P, width], F32, name=f"bank{first}")
            banks.append(bank)
            within = first % HALF_TOKENS
            nc.tensor.matmul_mx(
                out=bank[:],
                lhsT=q_codes[:].bitcast(FP8X4),
                lhsT_scale=q_scales[:],
                rhs=key_words[first // HALF_TOKENS][:, 2 * within : 2 * (within + width)].bitcast(FP4X4),
                rhs_scale=key_scales[:, first : first + width],
                start=True,
                stop=True,
            )
            if engine == "scalar":
                nc.scalar.activation(a[:, first : first + width], bank[:], ACT.Copy)
            else:
                nc.vector.tensor_copy(a[:, first : first + width], bank[:])

        by2 = [sb.tile([P, HALF_SLOTS], F32, name=f"by2_{h}") for h in range(2)]
        by3 = [sb.tile([P, HALF_SLOTS], F32, name=f"by3_{h}") for h in range(2)]
        w = sb.tile([P, I], F32, name="w")
        first_half, second_half = list_columns(0, HALF_SLOTS), list_columns(HALF_SLOTS, I)
        nc.vector.tensor_copy(by2[0][:], a[:].indirect(list2[:, first_half]))
        nc.scalar.activation(by3[0][:], a[:].indirect(list3[:, first_half]), ACT.Copy)
        nc.scalar.activation(by2[1][:], a[:].indirect(list2[:, second_half]), ACT.Copy)
        nc.scalar.activation(by3[1][:], a[:].indirect(list3[:, second_half]), ACT.Copy)

        nc.vector.tensor_tensor(w[:, 0:FIRST_SLOTS], by2[0][:, 0:FIRST_SLOTS], by3[0][:, 0:FIRST_SLOTS], ALU.max)
        nc.vector.tensor_tensor(w[:, FIRST_SLOTS:HALF_SLOTS], by2[0][:, FIRST_SLOTS:], by3[0][:, FIRST_SLOTS:], ALU.max)
        nc.vector.tensor_tensor(
            shadow[:].indirect(list1[:, list_columns(0, FIRST_SLOTS)]),
            w[:, 0:FIRST_SLOTS],
            lam_wide[:, 0:FIRST_SLOTS],
            ALU.mult,
        )
        nc.vector.tensor_tensor(w[:, HALF_SLOTS:], by2[1][:], by3[1][:], ALU.max)
        nc.vector.tensor_tensor(
            shadow[:].indirect(list1[:, list_columns(FIRST_SLOTS, I)]), w[:, FIRST_SLOTS:], lam_wide[:], ALU.mult
        )

        cc = sb.tile([P, T], F32, name="cc")
        nc.gpsimd.tensor_tensor(cc[:, VECTOR_COLUMNS:], a[:, VECTOR_COLUMNS:], shadow[:, VECTOR_COLUMNS:], ALU.subtract)
        second_first = PASSES[1][0]
        nc.vector.tensor_tensor(cc[:, 0:second_first], banks[0][:], shadow[:, 0:second_first], ALU.subtract)
        nc.vector.tensor_tensor(
            cc[:, second_first:VECTOR_COLUMNS],
            banks[1][:, 0 : VECTOR_COLUMNS - second_first],
            shadow[:, second_first:VECTOR_COLUMNS],
            ALU.subtract,
        )
        neg_top = sb.tile([P, 1], F32, name="neg_top")
        nc.vector.tensor_reduce(neg_top[:], cc[:], mybir.AxisListType.X, ALU.max, negate=True)

        for h, columns in enumerate((first_half, second_half)):
            y = sb.tile([P, HALF_SLOTS], F32, name=f"y_{h}")
            nc.scalar.activation(y[:], cc[:].indirect(list4[:, columns]), ACT.Exp, bias=neg_top[:])
            nc.sync.dma_start(out[:, h * HALF_SLOTS : (h + 1) * HALF_SLOTS], y[:])
